import numpy as np, ml_dtypes
CORES = [97,101,225,229,353,357,481,485]
N = 8
TK, LAY = 64, 3
def setup_inputs(rng):
    return {"x": rng.standard_normal((N, 128, TK), dtype=np.float32).astype(ml_dtypes.bfloat16), "wu": (rng.standard_normal((N, 128, LAY * 256), dtype=np.float32) / 16).astype(ml_dtypes.bfloat16), "wd": (rng.standard_normal((N, 128, 256), dtype=np.float32) / 16).astype(ml_dtypes.bfloat16)}
def setup_inputs_big(rng):
    d = setup_inputs(rng)
    for k in ("x",): d[k] = (d[k].astype(np.float32) * 1048576.0).astype(d[k].dtype)
    return d
def setup_inputs_small(rng):
    d = setup_inputs(rng)
    for k in ("x",): d[k] = (d[k].astype(np.float32) * (1 / 1048576.0)).astype(d[k].dtype)
    return d
def setup_inputs_apart(rng):
    d = setup_inputs(rng)
    f = (10.0 ** rng.permutation(np.linspace(-1.5, 1.5, N))).astype(np.float32).reshape(N, 1, 1)
    for k in ("x",): d[k] = (d[k].astype(np.float32) * f).astype(d[k].dtype)
    return d
def reference(x, wu, wd):
    X, WU, WD = x.astype(np.float64), wu.astype(np.float64), wd.astype(np.float64)
    s = list(X)
    for l in range(LAY):
        for q in range(0, N, 2 << l):
            p = q + (1 << l)
            s[q] = np.maximum(WU[q][:, 256 * l:256 * l + 128].T @ s[q] + WU[q][:, 256 * l + 128:256 * l + 256].T @ s[p], 0.0)
    for l in range(LAY - 1, -1, -1):
        for q in range(0, N, 2 << l):
            p = q + (1 << l)
            s[p] = np.maximum(WD[p][:, 0:128].T @ s[p] + WD[p][:, 128:256].T @ s[q], 0.0)
    return {"y": np.stack(s).astype(ml_dtypes.bfloat16)}

@@ -1,0 +1,273 @@
+from concourse.bass import DstId, RemoteDMATransfer
+from concourse.mybir import AluOpType
+
+TK = 64
+PK = 576
+
+SCRATCH = {
+    "pk": ("sbuf", [128, PK], "bfloat16"),
+    "ol": ("sbuf", [128, PK], "bfloat16"),
+    "lk": ("sbuf", [128, PK], "bfloat16"),
+    "xr": ("sbuf", [128, 2 * TK], "bfloat16"),
+    "wr": ("sbuf", [128, 256], "bfloat16"),
+    "w4": ("sbuf", [128, 256], "bfloat16"),
+    "ne": ("sbuf", [128, 128], "bfloat16"),
+    "zb": ("sbuf", [128, 128], "bfloat16"),
+    "zz": ("sbuf", [128, TK], "float32"),
+    "sa": ("sbuf", [128, 2 * TK], "bfloat16"),
+    "sb": ("sbuf", [128, TK], "bfloat16"),
+    "rb": ("sbuf", [128, TK], "bfloat16"),
+    "pp": ("sbuf", [128, TK], "bfloat16"),
+    "qq": ("sbuf", [128, TK], "bfloat16"),
+    "mn": ("sbuf", [128, TK], "bfloat16"),
+    "sc": ("sbuf", [128, TK], "bfloat16"),
+    "d1": ("sbuf", [128, TK], "bfloat16"),
+    "d2": ("sbuf", [128, TK], "bfloat16"),
+    "yb": ("sbuf", [128, TK], "bfloat16"),
+    "p0": ("psum", [128, 512], "float32"),
+    "p1": ("psum", [128, 512], "float32"),
+    "p2": ("psum", [128, 512], "float32"),
+    "p3": ("psum", [128, 512], "float32"),
+    "p4": ("psum", [128, 512], "float32"),
+    "p5": ("psum", [128, 512], "float32"),
+    "p6": ("psum", [128, 512], "float32"),
+}
+LOADS = ["lx", "lu", "lw", "lr", "st"]
+ARRIVALS = ["aol", "ax0", "ax1", "awr", "aw4", "alk", "asb", "arb", "app", "aqq"]
+ONES = ["zs", "zt", "vn", "vm", "vf"] + ["m%d" % i for i in range(7)] + ["v%d" % i for i in range(6)]
+SEMAPHORES = LOADS + ARRIVALS + ONES + ["sent"]
+
+
+def _bits(mask):
+    return [i for i in range(16) if (mask >> i) & 1]
+
+
+def _same_chip(topo, a, b):
+    return topo.host(a) == topo.host(b) and topo.chip(a) == topo.chip(b)
+
+
+def _lanes(topo, cores, src):
+    off = None
+    on = []
+    for d in cores:
+        if d == src or not topo.may_write(src, d):
+            continue
+        b = _bits(topo.mask(src, d))
+        if _same_chip(topo, src, d):
+            on = b
+        else:
+            off = b if off is None else [e for e in off if e in b]
+    h = len(off) // 2
+    only_on = [e for e in on if e not in off]
+    return {"lo": off[:h], "up": off[h:], "all": off, "hi": only_on[:h]}
+
+
+def _plan(topo, cores):
+    n = len(cores)
+    rack = [topo.rack(topo.host(c)) for c in cores]
+    far = [r for r in range(n) if not topo.may_write(cores[0], cores[r])]
+    calls = {r: [] for r in range(n)}
+
+    def reach(r):
+        return [s for s in range(n) if rack[s] != rack[r] and topo.may_write(cores[r], cores[s])]
+
+    for q0 in range(0, n, 4):
+        o0, q1, o1 = q0 + 1, q0 + 2, q0 + 3
+        calls[q0].append((["lx", "lu"], [(q1, ("pk", 0, PK), ("ol", 0, PK), "aol", "all")]))
+        calls[q1].append((["lx", "lu"], [(q0, ("pk", 0, 320), ("ol", 0, 320), "aol", "all")]))
+        calls[o0].append((["lx"], [(q0, ("pk", 0, TK), ("xr", 0, TK), "ax0", "hi"),
+                                   (q1, ("pk", 0, TK), ("xr", 0, TK), "ax0", "lo")]))
+        calls[o1].append((["lx"], [(q1, ("pk", 0, TK), ("xr", TK, 2 * TK), "ax1", "hi"),
+                                   (q0, ("pk", 0, TK), ("xr", TK, 2 * TK), "ax1", "lo")]))
+        if q0 == 0:
+            lead = [r for r in range(2, n, 2) if r not in far]
+            odd = [r for r in range(3, n, 2) if r not in far]
+            w = ("wr", 0, 256)
+            calls[0].append((["lr"], [(lead[0], w, w, "awr", "lo"), (lead[1], w, w, "awr", "up")]))
+            calls[0].append(([], [(odd[0], w, w, "awr", "lo"), (odd[1], w, w, "awr", "up"), (o0, w, w, "awr", "hi")]))
+        else:
+            w = ("w4", 0, 256)
+            calls[q0].append((["lw"], [(q1, w, w, "aw4", "lo"), (o1, w, w, "aw4", "up"), (o0, w, w, "aw4", "hi")]))
+        calls[q1].append((["lw"], [(o1, ("pk", 0, PK), ("lk", 0, PK), "alk", "hi")]))
+        s = ("sb", 0, TK)
+        for q, o in ((q0, o0), (q1, o1)):
+            t = reach(q)
+            if t[0] in far:
+                h = ("pp", 0, TK)
+                calls[q].append((["v2", "v5"], [(t[0], h, h, "app", "lo"), (t[1], h, h, "app", "up"),
+                                                (o, s, s, "asb", "hi")]))
+            else:
+                calls[q].append((["v2"], [(t[0], s, ("rb", 0, TK), "arb", "lo"), (t[1], s, ("rb", 0, TK), "arb", "up"),
+                                          (o, s, s, "asb", "hi")]))
+            if rack[q] == rack[far[0]] and q not in far:
+                h = ("qq", 0, TK)
+                calls[q].append((["v5"], [(far[0], h, h, "aqq", "lo"), (far[1], h, h, "aqq", "up")]))
+    return calls, far
+
+
+def rank_program(g, core, T, topo):
+    r = T.rank_of(core)
+    if r is None:
+        return
+    cores = list(T.cores)
+    S = T.sem
+    calls, far = _plan(topo, cores)
+
+    full = {s: 16 for s in LOADS}
+    full.update({s: 1 for s in ONES})
+    full.update({s: 0 for s in ARRIVALS})
+    for src in calls:
+        ln = _lanes(topo, cores, cores[src])
+        for _, trs in calls[src]:
+            for (dst, _, _, sem, lane) in trs:
+                if dst == r:
+                    full[sem] += len(ln[lane])
+
+    queues = {"g": g, "t": g.tensor, "v": g.vector, "s": g.sync}
+    seen = {}
+
+    def need(q, sems):
+        for s in sems:
+            if (q, s) not in seen:
+                seen[(q, s)] = True
+                queues[q].wait_ge(S[s], full[s])
+
+    def cols(name, c0, c1):
+        return T[name][:, c0:c1]
+
+    leader, q0, q1 = r % 2 == 0, r % 4 == 0, r % 4 == 2
+    o1 = r % 4 == 3
+    is_far = r in far
+    d4 = far[0]
+
+    g.sync.dma_start(cols("pk", 0, TK), T.x[:]).then_inc(S.lx, 16)
+    if q0:
+        g.scalar.dma_start(cols("pk", TK, PK), T.wu[:, 0:512]).then_inc(S.lu, 16)
+        if r == 0:
+            g.sync.dma_start(T.wr[:], T.wu[:, 512:768]).then_inc(S.lr, 16)
+        else:
+            g.sync.dma_start(T.w4[:], T.wd[:]).then_inc(S.lw, 16)
+    elif q1:
+        g.scalar.dma_start(cols("pk", TK, 320), T.wu[:, 0:256]).then_inc(S.lu, 16)
+        g.sync.dma_start(cols("pk", 320, PK), T.wd[:]).then_inc(S.lw, 16)
+    else:
+        g.scalar.dma_start(cols("pk", 320, PK), T.wd[:]).then_inc(S.lw, 16)
+
+    ln = _lanes(topo, cores, core)
+    sent = 0
+    for waits, trs in calls[r]:
+        need("g", waits)
+        lst = []
+        for (dst, a, b, sem, lane) in trs:
+            rid, pid = topo.addr(cores[dst], core)
+            m = 0
+            for e in ln[lane]:
+                m |= 1 << e
+            sent += len(ln[lane])
+            lst.append(RemoteDMATransfer(dst_ids=[DstId(rid=rid, pnc=pid)], dma_engine_mask=m, remote_sem=S[sem],
+                                         src=cols(*a), dst=cols(*b)))
+        g.remote_dma_fused(lst, local_sem=S.sent)
+    g.wait_ge(S.sent, sent)
+
+    g.vector.memset(T.zz[:], 0.0).then_inc(S.zs, 1)
+
+    def mm(ps, lhsT, rhs, start, stop, waits, done=None):
+        need("t", waits)
+        i = g.tensor.matmul(T[ps][:, 0:TK], lhsT, rhs, start, stop)
+        if done is not None:
+            i.then_inc(S[done], 1)
+
+    def relu(ps, out, msem, vsem):
+        need("v", [msem, "zs"])
+        g.vector.tensor_tensor(out, T[ps][:, 0:TK], T.zz[:], AluOpType.max).then_inc(S[vsem], 1)
+
+    X = cols("pk", 0, TK)
+    ownD, ownE = cols("pk", 320, 448), cols("pk", 448, PK)
+    wrU, wrV = cols("wr", 0, 128), cols("wr", 128, 256)
+    w4D, w4E = cols("w4", 0, 128), cols("w4", 128, 256)
+    swr = "lr" if r == 0 else "awr"
+    sw4 = "lw" if r == d4 else "aw4"
+    sb, rb, sc, d1, d2, yb = T.sb[:], T.rb[:], T.sc[:], T.d1[:], T.d2[:], T.yb[:]
+    ssb = "v2" if leader else "asb"
+
+    if is_far:
+        g.vector.memset(T.zb[:], 0.0).then_inc(S.zt, 1)
+        need("v", ["zt", sw4])
+        g.vector.tensor_tensor(T.ne[:], T.zb[:], w4E, AluOpType.subtract).then_inc(S.vn, 1)
+
+    if leader:
+        me, ot = (0, 1) if q0 else (1, 0)
+        sa_me, sa_ot = cols("sa", me * TK, me * TK + TK), cols("sa", ot * TK, ot * TK + TK)
+        l1 = "pk" if q0 else "ol"
+        U1, V1 = cols(l1, 320, 448), cols(l1, 448, PK)
+        w_me, w_ot = (U1, V1) if q0 else (V1, U1)
+        mm("p0", cols("pk", 64, 192), X, True, False, ["lx", "lu"])
+        mm("p0", cols("pk", 192, 320), cols("xr", me * TK, me * TK + TK), False, True, ["ax%d" % me], "m0")
+        relu("p0", sa_me, "m0", "v0")
+        mm("p1", cols("ol", 64, 192), cols("ol", 0, TK), True, False, ["aol"])
+        mm("p1", cols("ol", 192, 320), cols("xr", ot * TK, ot * TK + TK), False, True, ["ax%d" % ot], "m1")
+        relu("p1", sa_ot, "m1", "v1")
+        mm("p2", w_me, sa_me, True, False, ["v0"])
+        mm("p2", w_ot, sa_ot, False, True, ["v1"], "m2")
+        relu("p2", sb, "m2", "v2")
+
+    sends_p = leader and any(t[3] == "app" for _, trs in calls[r] for t in trs)
+    sends_q = leader and any(t[3] == "aqq" for _, trs in calls[r] for t in trs)
+
+    if not leader:
+        mm("p6", ownD, X, True, False, ["lx", "lw"])
+    if o1:
+        mm("p1", cols("lk", 64, 192), cols("lk", 0, TK), True, False, ["alk"])
+        mm("p1", cols("lk", 192, 320), X, False, True, [], "m1")
+        relu("p1", cols("sa", TK, 2 * TK), "m1", "v1")
+        mm("p5", cols("lk", 320, 448), cols("sa", TK, 2 * TK), True, False, ["v1"])
+
+    if sends_p:
+        mm("p5", wrU, sb, True, True, ["v2", swr], "m5")
+        need("v", ["m5", "zs"])
+        g.vector.tensor_tensor(T.pp[:], T.zz[:], T.p5[:, 0:TK], AluOpType.subtract).then_inc(S.v5, 1)
+    if sends_q:
+        mm("p5", wrV, sb, True, True, ["v2", swr], "m5")
+        need("v", ["m5"])
+        g.vector.tensor_copy(T.qq[:], T.p5[:, 0:TK]).then_inc(S.v5, 1)
+
+    in_root_rack = topo.rack(topo.host(core)) == topo.rack(topo.host(cores[0]))
+    last = None
+    if is_far:
+        mm("p4", w4D, sb, True, False, [ssb, sw4])
+        mm("p4", w4E, T.qq[:], False, False, ["aqq"])
+        need("v", ["app", "aqq"])
+        g.vector.tensor_tensor(T.mn[:], T.pp[:], T.qq[:], AluOpType.min).then_inc(S.vm, 1)
+        mm("p4", T.ne[:], T.mn[:], False, True, ["vm", "vn"], "m4")
+        if r == d4:
+            relu("p4", yb, "m4", "vf")
+        else:
+            relu("p4", d1, "m4", "v4")
+            last = (d1, "v4")
+    else:
+        w_own, w_oth = (wrU, wrV) if in_root_rack else (wrV, wrU)
+        mm("p3", w_own, sb, True, False, [ssb, swr])
+        if q1:
+            mm("p6", ownD, cols("sa", TK, 2 * TK), True, False, ["lw"])
+        mm("p3", w_oth, rb, False, True, ["arb"], "m3")
+        if r == 0:
+            relu("p3", yb, "m3", "vf")
+        else:
+            relu("p3", sc, "m3", "v3")
+            last = (sc, "v3")
+            if not in_root_rack:
+                mm("p4", w4D, sb, True, False, [sw4])
+                mm("p4", w4E, sc, False, True, ["v3"], "m4")
+                relu("p4", d1, "m4", "v4")
+                last = (d1, "v4")
+    if o1:
+        mm("p5", cols("lk", 448, PK), last[0], False, True, [last[1]], "m5")
+        relu("p5", d2, "m5", "v5")
+        last = (d2, "v5")
+    if last is not None:
+        mm("p6", ownE, last[0], False, True, [last[1]], "m6")
+        relu("p6", yb, "m6", "vf")
+
+    need("s", ["vf"])
+    g.sync.dma_start(T.y[:], yb).then_inc(S.st, 16)
+    g.sync.wait_ge(S.st, 16)

@@ -2,6 +2,7 @@ from concourse.bass import DstId, RemoteDMATransfer
 from concourse.mybir import AluOpType
 
 TK = 64
+XC = 256
 PK = 576
 
 SCRATCH = {
@@ -32,8 +33,8 @@ SCRATCH = {
     "p5": ("psum", [128, 512], "float32"),
     "p6": ("psum", [128, 512], "float32"),
 }
-LOADS = ["lx", "lu", "lw", "lr", "st"]
-ARRIVALS = ["aol", "ax0", "ax1", "awr", "aw4", "alk", "asb", "arb", "app", "aqq"]
+LOADS = ["lx", "lu", "lv", "lw", "lr", "st"]
+ARRIVALS = ["aol", "aob", "ax0", "ax1", "awr", "awu", "awv", "aw4", "alk", "ald", "asb", "arb", "app", "aqq"]
 ONES = ["zs", "zt", "vn", "vm", "vf"] + ["m%d" % i for i in range(7)] + ["v%d" % i for i in range(6)]
 SEMAPHORES = LOADS + ARRIVALS + ONES + ["sent"]
 
@@ -59,50 +60,53 @@ def _lanes(topo, cores, src):
             off = b if off is None else [e for e in off if e in b]
     h = len(off) // 2
     only_on = [e for e in on if e not in off]
-    return {"lo": off[:h], "up": off[h:], "all": off, "hi": only_on[:h]}
+    k = len(only_on) // 2
+    return {"lo": off[:h], "up": off[h:], "all": off, "hi": only_on, "h0": only_on[:k], "h1": only_on[k:]}
 
 
 def _plan(topo, cores):
     n = len(cores)
     rack = [topo.rack(topo.host(c)) for c in cores]
     far = [r for r in range(n) if not topo.may_write(cores[0], cores[r])]
+    qsrc = [r for r in range(0, n, 2) if rack[r] != rack[0] and r not in far][0]
     calls = {r: [] for r in range(n)}
 
     def reach(r):
         return [s for s in range(n) if rack[s] != rack[r] and topo.may_write(cores[r], cores[s])]
 
+    X = ("pk", XC, XC + TK)
+    U, V = ("wr", 0, 128), ("wr", 128, 256)
     for q0 in range(0, n, 4):
         o0, q1, o1 = q0 + 1, q0 + 2, q0 + 3
-        calls[q0].append((["lx", "lu"], [(q1, ("pk", 0, PK), ("ol", 0, PK), "aol", "all")]))
-        calls[q1].append((["lx", "lu"], [(q0, ("pk", 0, 320), ("ol", 0, 320), "aol", "all")]))
-        calls[o0].append((["lx"], [(q0, ("pk", 0, TK), ("xr", 0, TK), "ax0", "hi"),
-                                   (q1, ("pk", 0, TK), ("xr", 0, TK), "ax0", "lo")]))
-        calls[o1].append((["lx"], [(q1, ("pk", 0, TK), ("xr", TK, 2 * TK), "ax1", "hi"),
-                                   (q0, ("pk", 0, TK), ("xr", TK, 2 * TK), "ax1", "lo")]))
-        if q0 == 0:
-            lead = [r for r in range(2, n, 2) if r not in far]
-            odd = [r for r in range(3, n, 2) if r not in far]
-            w = ("wr", 0, 256)
-            calls[0].append((["lr"], [(lead[0], w, w, "awr", "lo"), (lead[1], w, w, "awr", "up")]))
-            calls[0].append(([], [(odd[0], w, w, "awr", "lo"), (odd[1], w, w, "awr", "up"), (o0, w, w, "awr", "hi")]))
+        root = rack[q0] == rack[0]
+        w, lw, aw = (("wr", 0, 256), "lr", "awr") if root else (("w4", 0, 256), "lw", "aw4")
+        calls[q0].append((["lu", lw], [(q1, ("pk", 0, XC), ("ol", 0, XC), "aol", "all"), (o0, w, w, aw, "hi")]))
+        calls[q0].append((["lx", "lv"], [(q1, ("pk", XC, PK), ("ol", XC, PK), "aob", "all")]))
+        calls[q1].append((["lx", "lu"], [(q0, ("pk", 0, 320), ("ol", 0, 320), "aol", "all"),
+                                         (o1, ("pk", 0, 320), ("lk", 0, 320), "alk", "hi")]))
+        calls[q1].append((["lw"], [(o1, ("pk", 320, PK), ("lk", 320, PK), "ald", "hi")]))
+        calls[o0].append((["lx"], [(q0, X, ("xr", 0, TK), "ax0", "h0"), (q1, X, ("xr", 0, TK), "ax0", "all")]))
+        calls[o1].append((["lx"], [(q1, X, ("xr", TK, 2 * TK), "ax1", "h0"), (q0, X, ("xr", TK, 2 * TK), "ax1", "all")]))
+        if root:
+            calls[o0].append((["awr"], [(q1, U, U, "awu", "lo"), (qsrc, V, V, "awv", "up")]))
+            calls[o0].append(([], [(q1, V, V, "awv", "lo"), (o1, V, V, "awv", "up")]))
+            calls[o0].append(([], [(o1, U, U, "awu", "all")]))
         else:
-            w = ("w4", 0, 256)
-            calls[q0].append((["lw"], [(q1, w, w, "aw4", "lo"), (o1, w, w, "aw4", "up"), (o0, w, w, "aw4", "hi")]))
-        calls[q1].append((["lw"], [(o1, ("pk", 0, PK), ("lk", 0, PK), "alk", "hi")]))
-        s = ("sb", 0, TK)
+            calls[o0].append((["aw4"], [(q1, w, w, "aw4", "lo"), (o1, w, w, "aw4", "up")]))
+        s, h, k = ("sb", 0, TK), ("pp", 0, TK), ("qq", 0, TK)
         for q, o in ((q0, o0), (q1, o1)):
             t = reach(q)
-            if t[0] in far:
-                h = ("pp", 0, TK)
+            if root:
                 calls[q].append((["v2", "v5"], [(t[0], h, h, "app", "lo"), (t[1], h, h, "app", "up"),
                                                 (o, s, s, "asb", "hi")]))
+            elif q == qsrc:
+                calls[q].append((["v2", "v5"], [(far[0], k, k, "aqq", "lo"), (far[1], k, k, "aqq", "up"),
+                                                (o, k, k, "aqq", "h0"), (o, s, s, "asb", "h1")]))
+                calls[q].append(([], [(t[0], s, ("rb", 0, TK), "arb", "lo"), (t[1], s, ("rb", 0, TK), "arb", "up")]))
             else:
                 calls[q].append((["v2"], [(t[0], s, ("rb", 0, TK), "arb", "lo"), (t[1], s, ("rb", 0, TK), "arb", "up"),
                                           (o, s, s, "asb", "hi")]))
-            if rack[q] == rack[far[0]] and q not in far:
-                h = ("qq", 0, TK)
-                calls[q].append((["v5"], [(far[0], h, h, "aqq", "lo"), (far[1], h, h, "aqq", "up")]))
-    return calls, far
+    return calls, far, qsrc
 
 
 def rank_program(g, core, T, topo):
@@ -111,7 +115,7 @@ def rank_program(g, core, T, topo):
         return
     cores = list(T.cores)
     S = T.sem
-    calls, far = _plan(topo, cores)
+    calls, far, qsrc = _plan(topo, cores)
 
     full = {s: 16 for s in LOADS}
     full.update({s: 1 for s in ONES})
@@ -137,20 +141,24 @@ def rank_program(g, core, T, topo):
 
     leader, q0, q1 = r % 2 == 0, r % 4 == 0, r % 4 == 2
     o1 = r % 4 == 3
-    is_far = r in far
+    root_rack = topo.rack(topo.host(core)) == topo.rack(topo.host(cores[0]))
     d4 = far[0]
+    X = cols("pk", XC, XC + TK)
 
-    g.sync.dma_start(cols("pk", 0, TK), T.x[:]).then_inc(S.lx, 16)
     if q0:
-        g.scalar.dma_start(cols("pk", TK, PK), T.wu[:, 0:512]).then_inc(S.lu, 16)
         if r == 0:
             g.sync.dma_start(T.wr[:], T.wu[:, 512:768]).then_inc(S.lr, 16)
         else:
             g.sync.dma_start(T.w4[:], T.wd[:]).then_inc(S.lw, 16)
+        g.scalar.dma_start(cols("pk", 0, XC), T.wu[:, 0:256]).then_inc(S.lu, 16)
+        g.sync.dma_start(X, T.x[:]).then_inc(S.lx, 16)
+        g.scalar.dma_start(cols("pk", 320, PK), T.wu[:, 256:512]).then_inc(S.lv, 16)
     elif q1:
-        g.scalar.dma_start(cols("pk", TK, 320), T.wu[:, 0:256]).then_inc(S.lu, 16)
+        g.sync.dma_start(X, T.x[:]).then_inc(S.lx, 16)
+        g.scalar.dma_start(cols("pk", 0, XC), T.wu[:, 0:256]).then_inc(S.lu, 16)
         g.sync.dma_start(cols("pk", 320, PK), T.wd[:]).then_inc(S.lw, 16)
     else:
+        g.sync.dma_start(X, T.x[:]).then_inc(S.lx, 16)
         g.scalar.dma_start(cols("pk", 320, PK), T.wd[:]).then_inc(S.lw, 16)
 
     ln = _lanes(topo, cores, core)
@@ -170,6 +178,8 @@ def rank_program(g, core, T, topo):
     g.wait_ge(S.sent, sent)
 
     g.vector.memset(T.zz[:], 0.0).then_inc(S.zs, 1)
+    if not root_rack:
+        g.vector.memset(T.zb[:], 0.0).then_inc(S.zt, 1)
 
     def mm(ps, lhsT, rhs, start, stop, waits, done=None):
         need("t", waits)
@@ -181,62 +191,65 @@ def rank_program(g, core, T, topo):
         need("v", [msem, "zs"])
         g.vector.tensor_tensor(out, T[ps][:, 0:TK], T.zz[:], AluOpType.max).then_inc(S[vsem], 1)
 
-    X = cols("pk", 0, TK)
     ownD, ownE = cols("pk", 320, 448), cols("pk", 448, PK)
     wrU, wrV = cols("wr", 0, 128), cols("wr", 128, 256)
     w4D, w4E = cols("w4", 0, 128), cols("w4", 128, 256)
-    swr = "lr" if r == 0 else "awr"
+    whole = "lr" if r == 0 else ("awr" if full["awr"] else None)
+    swu, swv = whole or "awu", whole or "awv"
     sw4 = "lw" if r == d4 else "aw4"
     sb, rb, sc, d1, d2, yb = T.sb[:], T.rb[:], T.sc[:], T.d1[:], T.d2[:], T.yb[:]
     ssb = "v2" if leader else "asb"
-
-    if is_far:
-        g.vector.memset(T.zb[:], 0.0).then_inc(S.zt, 1)
-        need("v", ["zt", sw4])
-        g.vector.tensor_tensor(T.ne[:], T.zb[:], w4E, AluOpType.subtract).then_inc(S.vn, 1)
+    a_q1 = cols("sa", TK, 2 * TK)
 
     if leader:
         me, ot = (0, 1) if q0 else (1, 0)
         sa_me, sa_ot = cols("sa", me * TK, me * TK + TK), cols("sa", ot * TK, ot * TK + TK)
-        l1 = "pk" if q0 else "ol"
+        l1, s1 = ("pk", "lv") if q0 else ("ol", "aob")
         U1, V1 = cols(l1, 320, 448), cols(l1, 448, PK)
         w_me, w_ot = (U1, V1) if q0 else (V1, U1)
-        mm("p0", cols("pk", 64, 192), X, True, False, ["lx", "lu"])
-        mm("p0", cols("pk", 192, 320), cols("xr", me * TK, me * TK + TK), False, True, ["ax%d" % me], "m0")
+        mm("p0", cols("pk", 0, 128), X, True, False, ["lx", "lu"])
+        mm("p0", cols("pk", 128, 256), cols("xr", me * TK, me * TK + TK), False, True, ["ax%d" % me], "m0")
         relu("p0", sa_me, "m0", "v0")
-        mm("p1", cols("ol", 64, 192), cols("ol", 0, TK), True, False, ["aol"])
-        mm("p1", cols("ol", 192, 320), cols("xr", ot * TK, ot * TK + TK), False, True, ["ax%d" % ot], "m1")
+        mm("p1", cols("ol", 0, 128), cols("ol", XC, XC + TK), True, False, ["aol"] if q0 else ["aol", "aob"])
+        mm("p1", cols("ol", 128, 256), cols("xr", ot * TK, ot * TK + TK), False, True, ["ax%d" % ot], "m1")
         relu("p1", sa_ot, "m1", "v1")
-        mm("p2", w_me, sa_me, True, False, ["v0"])
+        mm("p2", w_me, sa_me, True, False, ["v0", s1])
         mm("p2", w_ot, sa_ot, False, True, ["v1"], "m2")
         relu("p2", sb, "m2", "v2")
-
-    sends_p = leader and any(t[3] == "app" for _, trs in calls[r] for t in trs)
-    sends_q = leader and any(t[3] == "aqq" for _, trs in calls[r] for t in trs)
-
-    if not leader:
+        if root_rack:
+            mm("p5", wrU, sb, True, True, ["v2", swu], "m5")
+            need("v", ["m5", "zs"])
+            g.vector.tensor_tensor(T.pp[:], T.zz[:], T.p5[:, 0:TK], AluOpType.subtract).then_inc(S.v5, 1)
+        elif r == qsrc:
+            mm("p5", wrV, sb, True, True, ["v2", swv], "m5")
+            need("v", ["m5"])
+            g.vector.tensor_copy(T.qq[:], T.p5[:, 0:TK]).then_inc(S.v5, 1)
+        if q1:
+            mm("p6", ownD, a_q1, True, False, ["lw"])
+    else:
         mm("p6", ownD, X, True, False, ["lx", "lw"])
     if o1:
-        mm("p1", cols("lk", 64, 192), cols("lk", 0, TK), True, False, ["alk"])
-        mm("p1", cols("lk", 192, 320), X, False, True, [], "m1")
-        relu("p1", cols("sa", TK, 2 * TK), "m1", "v1")
-        mm("p5", cols("lk", 320, 448), cols("sa", TK, 2 * TK), True, False, ["v1"])
+        mm("p1", cols("lk", 0, 128), cols("lk", XC, XC + TK), True, False, ["alk"])
+        mm("p1", cols("lk", 128, 256), X, False, True, [], "m1")
+        relu("p1", a_q1, "m1", "v1")
+        mm("p5", cols("lk", 320, 448), a_q1, True, False, ["v1", "ald"])
 
-    if sends_p:
-        mm("p5", wrU, sb, True, True, ["v2", swr], "m5")
-        need("v", ["m5", "zs"])
-        g.vector.tensor_tensor(T.pp[:], T.zz[:], T.p5[:, 0:TK], AluOpType.subtract).then_inc(S.v5, 1)
-    if sends_q:
-        mm("p5", wrV, sb, True, True, ["v2", swr], "m5")
-        need("v", ["m5"])
-        g.vector.tensor_copy(T.qq[:], T.p5[:, 0:TK]).then_inc(S.v5, 1)
-
-    in_root_rack = topo.rack(topo.host(core)) == topo.rack(topo.host(cores[0]))
     last = None
-    if is_far:
+    if root_rack:
+        mm("p3", wrU, sb, True, False, [ssb, swu])
+        mm("p3", wrV, rb, False, True, ["arb", swv], "m3")
+        if r == 0:
+            relu("p3", yb, "m3", "vf")
+        else:
+            relu("p3", sc, "m3", "v3")
+            last = (sc, "v3")
+    else:
+        sqq = "v5" if r == qsrc else "aqq"
         mm("p4", w4D, sb, True, False, [ssb, sw4])
-        mm("p4", w4E, T.qq[:], False, False, ["aqq"])
-        need("v", ["app", "aqq"])
+        mm("p4", w4E, T.qq[:], False, False, [sqq])
+        need("v", ["zt", sw4])
+        g.vector.tensor_tensor(T.ne[:], T.zb[:], w4E, AluOpType.subtract).then_inc(S.vn, 1)
+        need("v", ["app", sqq])
         g.vector.tensor_tensor(T.mn[:], T.pp[:], T.qq[:], AluOpType.min).then_inc(S.vm, 1)
         mm("p4", T.ne[:], T.mn[:], False, True, ["vm", "vn"], "m4")
         if r == d4:
@@ -244,22 +257,6 @@ def rank_program(g, core, T, topo):
         else:
             relu("p4", d1, "m4", "v4")
             last = (d1, "v4")
-    else:
-        w_own, w_oth = (wrU, wrV) if in_root_rack else (wrV, wrU)
-        mm("p3", w_own, sb, True, False, [ssb, swr])
-        if q1:
-            mm("p6", ownD, cols("sa", TK, 2 * TK), True, False, ["lw"])
-        mm("p3", w_oth, rb, False, True, ["arb"], "m3")
-        if r == 0:
-            relu("p3", yb, "m3", "vf")
-        else:
-            relu("p3", sc, "m3", "v3")
-            last = (sc, "v3")
-            if not in_root_rack:
-                mm("p4", w4D, sb, True, False, [sw4])
-                mm("p4", w4E, sc, False, True, ["v3"], "m4")
-                relu("p4", d1, "m4", "v4")
-                last = (d1, "v4")
     if o1:
         mm("p5", cols("lk", 448, PK), last[0], False, True, [last[1]], "m5")
         relu("p5", d2, "m5", "v5")

@@ -2,25 +2,24 @@ from concourse.bass import DstId, RemoteDMATransfer
 from concourse.mybir import AluOpType
 
 TK = 64
-XC = 256
+GC = 256
 PK = 576
 
 SCRATCH = {
     "pk": ("sbuf", [128, PK], "bfloat16"),
+    "xo": ("sbuf", [128, TK], "bfloat16"),
     "ol": ("sbuf", [128, PK], "bfloat16"),
     "lk": ("sbuf", [128, PK], "bfloat16"),
     "xr": ("sbuf", [128, 2 * TK], "bfloat16"),
     "wr": ("sbuf", [128, 256], "bfloat16"),
     "w4": ("sbuf", [128, 256], "bfloat16"),
-    "ne": ("sbuf", [128, 128], "bfloat16"),
-    "zb": ("sbuf", [128, 128], "bfloat16"),
+    "one": ("sbuf", [128, 128], "bfloat16"),
+    "idm": ("sbuf", [128, 128], "bfloat16"),
     "zz": ("sbuf", [128, TK], "float32"),
     "sa": ("sbuf", [128, 2 * TK], "bfloat16"),
     "sb": ("sbuf", [128, TK], "bfloat16"),
-    "rb": ("sbuf", [128, TK], "bfloat16"),
+    "b4": ("sbuf", [128, TK], "bfloat16"),
     "pp": ("sbuf", [128, TK], "bfloat16"),
-    "qq": ("sbuf", [128, TK], "bfloat16"),
-    "mn": ("sbuf", [128, TK], "bfloat16"),
     "sc": ("sbuf", [128, TK], "bfloat16"),
     "d1": ("sbuf", [128, TK], "bfloat16"),
     "d2": ("sbuf", [128, TK], "bfloat16"),
@@ -32,10 +31,11 @@ SCRATCH = {
     "p4": ("psum", [128, 512], "float32"),
     "p5": ("psum", [128, 512], "float32"),
     "p6": ("psum", [128, 512], "float32"),
+    "p7": ("psum", [128, 512], "float32"),
 }
 LOADS = ["lx", "lu", "lv", "lw", "lr", "st"]
-ARRIVALS = ["aol", "aob", "ax0", "ax1", "awr", "awu", "awv", "aw4", "alk", "ald", "asb", "arb", "app", "aqq"]
-ONES = ["zs", "zt", "vn", "vm", "vf"] + ["m%d" % i for i in range(7)] + ["v%d" % i for i in range(6)]
+ARRIVALS = ["aid", "aol", "aob", "ax0", "ax1", "awr", "awu", "awv", "aw4", "alk", "ald", "ab4", "app"]
+ONES = ["zs", "on1", "idn", "mg", "vg", "vf"] + ["m%d" % i for i in range(7)] + ["v%d" % i for i in range(6)]
 SEMAPHORES = LOADS + ARRIVALS + ONES + ["sent"]
 
 
@@ -60,53 +60,49 @@ def _lanes(topo, cores, src):
             off = b if off is None else [e for e in off if e in b]
     h = len(off) // 2
     only_on = [e for e in on if e not in off]
-    k = len(only_on) // 2
-    return {"lo": off[:h], "up": off[h:], "all": off, "hi": only_on, "h0": only_on[:k], "h1": only_on[k:]}
+    return {"lo": off[:h], "up": off[h:], "all": off, "chip": on, "hi": only_on, "h0": only_on[:len(only_on) // 2]}
 
 
 def _plan(topo, cores):
     n = len(cores)
     rack = [topo.rack(topo.host(c)) for c in cores]
     far = [r for r in range(n) if not topo.may_write(cores[0], cores[r])]
-    qsrc = [r for r in range(0, n, 2) if rack[r] != rack[0] and r not in far][0]
     calls = {r: [] for r in range(n)}
 
     def reach(r):
         return [s for s in range(n) if rack[s] != rack[r] and topo.may_write(cores[r], cores[s])]
 
-    X = ("pk", XC, XC + TK)
+    near_q, relay = reach(0)
+    X = ("xo", 0, TK)
+    EYE = ("idm", 0, 128)
     U, V = ("wr", 0, 128), ("wr", 128, 256)
     for q0 in range(0, n, 4):
         o0, q1, o1 = q0 + 1, q0 + 2, q0 + 3
         root = rack[q0] == rack[0]
         w, lw, aw = (("wr", 0, 256), "lr", "awr") if root else (("w4", 0, 256), "lw", "aw4")
-        calls[q0].append((["lu", lw], [(q1, ("pk", 0, XC), ("ol", 0, XC), "aol", "all"), (o0, w, w, aw, "hi")]))
-        calls[q0].append((["lx", "lv"], [(q1, ("pk", XC, PK), ("ol", XC, PK), "aob", "all")]))
-        calls[q1].append((["lx", "lu"], [(q0, ("pk", 0, 320), ("ol", 0, 320), "aol", "all"),
-                                         (o1, ("pk", 0, 320), ("lk", 0, 320), "alk", "hi")]))
+        calls[q0].append((["idn"], [(o0, EYE, EYE, "aid", "chip")]))
+        calls[q1].append((["idn"], [(o1, EYE, EYE, "aid", "chip")]))
+        calls[q0].append((["lv", lw], [(q1, ("pk", 320, PK), ("ol", 320, PK), "aob", "all"), (o0, w, w, aw, "hi")]))
+        calls[q0].append((["lu", "vg"], [(q1, ("pk", 128, 320), ("ol", 128, 320), "aol", "all")]))
+        if root:
+            calls[q0].append(([], [(relay, V, V, "awv", "all")]))
+        calls[q1].append((["lu", "vg"], [(q0, ("pk", 128, 320), ("ol", 128, 320), "aol", "all"),
+                                         (o1, ("pk", 128, 320), ("lk", 128, 320), "alk", "hi")]))
         calls[q1].append((["lw"], [(o1, ("pk", 320, PK), ("lk", 320, PK), "ald", "hi")]))
         calls[o0].append((["lx"], [(q0, X, ("xr", 0, TK), "ax0", "h0"), (q1, X, ("xr", 0, TK), "ax0", "all")]))
         calls[o1].append((["lx"], [(q1, X, ("xr", TK, 2 * TK), "ax1", "h0"), (q0, X, ("xr", TK, 2 * TK), "ax1", "all")]))
         if root:
-            calls[o0].append((["awr"], [(q1, U, U, "awu", "lo"), (qsrc, V, V, "awv", "up")]))
+            calls[o0].append((["awr"], [(q1, U, U, "awu", "all")]))
             calls[o0].append(([], [(q1, V, V, "awv", "lo"), (o1, V, V, "awv", "up")]))
-            calls[o0].append(([], [(o1, U, U, "awu", "all")]))
         else:
             calls[o0].append((["aw4"], [(q1, w, w, "aw4", "lo"), (o1, w, w, "aw4", "up")]))
-        s, h, k = ("sb", 0, TK), ("pp", 0, TK), ("qq", 0, TK)
         for q, o in ((q0, o0), (q1, o1)):
             t = reach(q)
-            if root:
-                calls[q].append((["v2", "v5"], [(t[0], h, h, "app", "lo"), (t[1], h, h, "app", "up"),
-                                                (o, s, s, "asb", "hi")]))
-            elif q == qsrc:
-                calls[q].append((["v2", "v5"], [(far[0], k, k, "aqq", "lo"), (far[1], k, k, "aqq", "up"),
-                                                (o, k, k, "aqq", "h0"), (o, s, s, "asb", "h1")]))
-                calls[q].append(([], [(t[0], s, ("rb", 0, TK), "arb", "lo"), (t[1], s, ("rb", 0, TK), "arb", "up")]))
-            else:
-                calls[q].append((["v2"], [(t[0], s, ("rb", 0, TK), "arb", "lo"), (t[1], s, ("rb", 0, TK), "arb", "up"),
-                                          (o, s, s, "asb", "hi")]))
-    return calls, far, qsrc
+            a, b, sem, wt = (("pp", 0, TK), ("pp", 0, TK), "app", "v5") if root else (("sb", 0, TK), ("b4", 0, TK), "ab4", "v2")
+            calls[q].append(([wt], [(t[0], a, b, sem, "lo"), (t[1], a, b, sem, "up"), (o, a, b, sem, "hi")]))
+    calls[relay].append((["awv"], [(far[1], V, V, "awv", "all"), (near_q, V, V, "awv", "hi")]))
+    calls[relay].append(([], [(far[0], V, V, "awv", "all")]))
+    return calls, far
 
 
 def rank_program(g, core, T, topo):
@@ -115,7 +111,7 @@ def rank_program(g, core, T, topo):
         return
     cores = list(T.cores)
     S = T.sem
-    calls, far, qsrc = _plan(topo, cores)
+    calls, far = _plan(topo, cores)
 
     full = {s: 16 for s in LOADS}
     full.update({s: 1 for s in ONES})
@@ -143,23 +139,30 @@ def rank_program(g, core, T, topo):
     o1 = r % 4 == 3
     root_rack = topo.rack(topo.host(core)) == topo.rack(topo.host(cores[0]))
     d4 = far[0]
-    X = cols("pk", XC, XC + TK)
+    X = T.xo[:]
 
     if q0:
         if r == 0:
             g.sync.dma_start(T.wr[:], T.wu[:, 512:768]).then_inc(S.lr, 16)
         else:
             g.sync.dma_start(T.w4[:], T.wd[:]).then_inc(S.lw, 16)
-        g.scalar.dma_start(cols("pk", 0, XC), T.wu[:, 0:256]).then_inc(S.lu, 16)
-        g.sync.dma_start(X, T.x[:]).then_inc(S.lx, 16)
         g.scalar.dma_start(cols("pk", 320, PK), T.wu[:, 256:512]).then_inc(S.lv, 16)
+        g.sync.dma_start(X, T.x[:]).then_inc(S.lx, 16)
+        g.scalar.dma_start(cols("pk", 0, GC), T.wu[:, 0:256]).then_inc(S.lu, 16)
     elif q1:
         g.sync.dma_start(X, T.x[:]).then_inc(S.lx, 16)
-        g.scalar.dma_start(cols("pk", 0, XC), T.wu[:, 0:256]).then_inc(S.lu, 16)
+        g.scalar.dma_start(cols("pk", 0, GC), T.wu[:, 0:256]).then_inc(S.lu, 16)
         g.sync.dma_start(cols("pk", 320, PK), T.wd[:]).then_inc(S.lw, 16)
     else:
         g.sync.dma_start(X, T.x[:]).then_inc(S.lx, 16)
         g.scalar.dma_start(cols("pk", 320, PK), T.wd[:]).then_inc(S.lw, 16)
+
+    if leader:
+        g.vector.memset(T.one[:], 1.0).then_inc(S.on1, 1)
+        need("g", ["on1"])
+        g.affine_select(T.idm[:], T.one[:], [[-1, 128]], AluOpType.is_equal, 0.0, 0, 1).then_inc(S.idn, 1)
+    g.vector.memset(T.zz[:], 0.0).then_inc(S.zs, 1)
+    seye = "idn" if leader else "aid"
 
     ln = _lanes(topo, cores, core)
     sent = 0
@@ -177,10 +180,6 @@ def rank_program(g, core, T, topo):
         g.remote_dma_fused(lst, local_sem=S.sent)
     g.wait_ge(S.sent, sent)
 
-    g.vector.memset(T.zz[:], 0.0).then_inc(S.zs, 1)
-    if not root_rack:
-        g.vector.memset(T.zb[:], 0.0).then_inc(S.zt, 1)
-
     def mm(ps, lhsT, rhs, start, stop, waits, done=None):
         need("t", waits)
         i = g.tensor.matmul(T[ps][:, 0:TK], lhsT, rhs, start, stop)
@@ -191,14 +190,14 @@ def rank_program(g, core, T, topo):
         need("v", [msem, "zs"])
         g.vector.tensor_tensor(out, T[ps][:, 0:TK], T.zz[:], AluOpType.max).then_inc(S[vsem], 1)
 
+    eye = T.idm[:]
     ownD, ownE = cols("pk", 320, 448), cols("pk", 448, PK)
     wrU, wrV = cols("wr", 0, 128), cols("wr", 128, 256)
     w4D, w4E = cols("w4", 0, 128), cols("w4", 128, 256)
     whole = "lr" if r == 0 else ("awr" if full["awr"] else None)
     swu, swv = whole or "awu", whole or "awv"
     sw4 = "lw" if r == d4 else "aw4"
-    sb, rb, sc, d1, d2, yb = T.sb[:], T.rb[:], T.sc[:], T.d1[:], T.d2[:], T.yb[:]
-    ssb = "v2" if leader else "asb"
+    sb, pp, sc, d1, d2, yb = T.sb[:], T.pp[:], T.sc[:], T.d1[:], T.d2[:], T.yb[:]
     a_q1 = cols("sa", TK, 2 * TK)
 
     if leader:
@@ -207,10 +206,13 @@ def rank_program(g, core, T, topo):
         l1, s1 = ("pk", "lv") if q0 else ("ol", "aob")
         U1, V1 = cols(l1, 320, 448), cols(l1, 448, PK)
         w_me, w_ot = (U1, V1) if q0 else (V1, U1)
-        mm("p0", cols("pk", 0, 128), X, True, False, ["lx", "lu"])
+        mm("p7", cols("pk", 0, 128), X, True, True, ["lx", "lu"], "mg")
+        need("v", ["mg"])
+        g.vector.tensor_copy(cols("pk", GC, GC + TK), T.p7[:, 0:TK]).then_inc(S.vg, 1)
+        mm("p0", cols("pk", 0, 128), X, True, False, [])
         mm("p0", cols("pk", 128, 256), cols("xr", me * TK, me * TK + TK), False, True, ["ax%d" % me], "m0")
         relu("p0", sa_me, "m0", "v0")
-        mm("p1", cols("ol", 0, 128), cols("ol", XC, XC + TK), True, False, ["aol"] if q0 else ["aol", "aob"])
+        mm("p1", eye, cols("ol", GC, GC + TK), True, False, [seye, "aol"])
         mm("p1", cols("ol", 128, 256), cols("xr", ot * TK, ot * TK + TK), False, True, ["ax%d" % ot], "m1")
         relu("p1", sa_ot, "m1", "v1")
         mm("p2", w_me, sa_me, True, False, ["v0", s1])
@@ -218,42 +220,41 @@ def rank_program(g, core, T, topo):
         relu("p2", sb, "m2", "v2")
         if root_rack:
             mm("p5", wrU, sb, True, True, ["v2", swu], "m5")
-            need("v", ["m5", "zs"])
-            g.vector.tensor_tensor(T.pp[:], T.zz[:], T.p5[:, 0:TK], AluOpType.subtract).then_inc(S.v5, 1)
-        elif r == qsrc:
-            mm("p5", wrV, sb, True, True, ["v2", swv], "m5")
             need("v", ["m5"])
-            g.vector.tensor_copy(T.qq[:], T.p5[:, 0:TK]).then_inc(S.v5, 1)
+            g.vector.tensor_copy(pp, T.p5[:, 0:TK]).then_inc(S.v5, 1)
         if q1:
             mm("p6", ownD, a_q1, True, False, ["lw"])
     else:
         mm("p6", ownD, X, True, False, ["lx", "lw"])
     if o1:
-        mm("p1", cols("lk", 0, 128), cols("lk", XC, XC + TK), True, False, ["alk"])
+        mm("p1", eye, cols("lk", GC, GC + TK), True, False, [seye, "alk"])
         mm("p1", cols("lk", 128, 256), X, False, True, [], "m1")
         relu("p1", a_q1, "m1", "v1")
         mm("p5", cols("lk", 320, 448), a_q1, True, False, ["v1", "ald"])
 
-    last = None
+    own_b4 = leader and not root_rack
+    b4, sb4 = (sb, "v2") if own_b4 else (T.b4[:], "ab4")
     if root_rack:
-        mm("p3", wrU, sb, True, False, [ssb, swu])
-        mm("p3", wrV, rb, False, True, ["arb", swv], "m3")
-        if r == 0:
-            relu("p3", yb, "m3", "vf")
+        if leader:
+            mm("p3", wrU, sb, True, False, ["v2", swu])
         else:
-            relu("p3", sc, "m3", "v3")
-            last = (sc, "v3")
+            mm("p3", eye, pp, True, False, [seye, "app"])
+        mm("p3", wrV, b4, False, True, [sb4, swv], "m3")
     else:
-        sqq = "v5" if r == qsrc else "aqq"
-        mm("p4", w4D, sb, True, False, [ssb, sw4])
-        mm("p4", w4E, T.qq[:], False, False, [sqq])
-        need("v", ["zt", sw4])
-        g.vector.tensor_tensor(T.ne[:], T.zb[:], w4E, AluOpType.subtract).then_inc(S.vn, 1)
-        need("v", ["app", sqq])
-        g.vector.tensor_tensor(T.mn[:], T.pp[:], T.qq[:], AluOpType.min).then_inc(S.vm, 1)
-        mm("p4", T.ne[:], T.mn[:], False, True, ["vm", "vn"], "m4")
+        mm("p3", wrV, b4, True, False, [sb4, swv])
+        mm("p3", eye, pp, False, True, [seye, "app"], "m3")
+    last = None
+    if r == 0:
+        relu("p3", yb, "m3", "vf")
+    else:
+        relu("p3", sc, "m3", "v3")
+        last = (sc, "v3")
+    if not root_rack:
+        mm("p4", w4D, b4, True, False, [sw4])
+        mm("p4", w4E, sc, False, True, ["v3"], "m4")
         if r == d4:
             relu("p4", yb, "m4", "vf")
+            last = None
         else:
             relu("p4", d1, "m4", "v4")
             last = (d1, "v4")

from concourse.bass import DstId, RemoteDMATransfer
from concourse.mybir import AluOpType

TK = 64
GC = 256
PK = 576

SCRATCH = {
    "pk": ("sbuf", [128, PK], "bfloat16"),
    "xo": ("sbuf", [128, TK], "bfloat16"),
    "ol": ("sbuf", [128, PK], "bfloat16"),
    "lk": ("sbuf", [128, PK], "bfloat16"),
    "xr": ("sbuf", [128, 2 * TK], "bfloat16"),
    "wr": ("sbuf", [128, 256], "bfloat16"),
    "w4": ("sbuf", [128, 256], "bfloat16"),
    "one": ("sbuf", [128, 128], "bfloat16"),
    "idm": ("sbuf", [128, 128], "bfloat16"),
    "zz": ("sbuf", [128, TK], "float32"),
    "sa": ("sbuf", [128, 2 * TK], "bfloat16"),
    "sb": ("sbuf", [128, TK], "bfloat16"),
    "b4": ("sbuf", [128, TK], "bfloat16"),
    "pp": ("sbuf", [128, TK], "bfloat16"),
    "sc": ("sbuf", [128, TK], "bfloat16"),
    "d1": ("sbuf", [128, TK], "bfloat16"),
    "d2": ("sbuf", [128, TK], "bfloat16"),
    "yb": ("sbuf", [128, TK], "bfloat16"),
    "p0": ("psum", [128, 512], "float32"),
    "p1": ("psum", [128, 512], "float32"),
    "p2": ("psum", [128, 512], "float32"),
    "p3": ("psum", [128, 512], "float32"),
    "p4": ("psum", [128, 512], "float32"),
    "p5": ("psum", [128, 512], "float32"),
    "p6": ("psum", [128, 512], "float32"),
    "p7": ("psum", [128, 512], "float32"),
}
LOADS = ["lx", "lu", "lv", "lw", "lr", "st"]
ARRIVALS = ["aid", "aol", "aob", "ax0", "ax1", "awr", "awu", "awv", "aw4", "alk", "ald", "ab4", "app"]
ONES = ["zs", "on1", "idn", "mg", "vg", "vf"] + ["m%d" % i for i in range(7)] + ["v%d" % i for i in range(6)]
SEMAPHORES = LOADS + ARRIVALS + ONES + ["sent"]


def _bits(mask):
    return [i for i in range(16) if (mask >> i) & 1]


def _same_chip(topo, a, b):
    return topo.host(a) == topo.host(b) and topo.chip(a) == topo.chip(b)


def _lanes(topo, cores, src):
    off = None
    on = []
    for d in cores:
        if d == src or not topo.may_write(src, d):
            continue
        b = _bits(topo.mask(src, d))
        if _same_chip(topo, src, d):
            on = b
        else:
            off = b if off is None else [e for e in off if e in b]
    h = len(off) // 2
    only_on = [e for e in on if e not in off]
    return {"lo": off[:h], "up": off[h:], "all": off, "chip": on, "hi": only_on, "h0": only_on[:len(only_on) // 2]}


def _plan(topo, cores):
    n = len(cores)
    rack = [topo.rack(topo.host(c)) for c in cores]
    far = [r for r in range(n) if not topo.may_write(cores[0], cores[r])]
    calls = {r: [] for r in range(n)}

    def reach(r):
        return [s for s in range(n) if rack[s] != rack[r] and topo.may_write(cores[r], cores[s])]

    near_q, relay = reach(0)
    X = ("xo", 0, TK)
    EYE = ("idm", 0, 128)
    U, V = ("wr", 0, 128), ("wr", 128, 256)
    for q0 in range(0, n, 4):
        o0, q1, o1 = q0 + 1, q0 + 2, q0 + 3
        root = rack[q0] == rack[0]
        w, lw, aw = (("wr", 0, 256), "lr", "awr") if root else (("w4", 0, 256), "lw", "aw4")
        calls[q0].append((["idn"], [(o0, EYE, EYE, "aid", "chip")]))
        calls[q1].append((["idn"], [(o1, EYE, EYE, "aid", "chip")]))
        calls[q0].append((["lv", lw], [(q1, ("pk", 320, PK), ("ol", 320, PK), "aob", "all"), (o0, w, w, aw, "hi")]))
        calls[q0].append((["lu", "vg"], [(q1, ("pk", 128, 320), ("ol", 128, 320), "aol", "all")]))
        if root:
            calls[q0].append(([], [(relay, V, V, "awv", "all")]))
        calls[q1].append((["lu", "vg"], [(q0, ("pk", 128, 320), ("ol", 128, 320), "aol", "all"),
                                         (o1, ("pk", 128, 320), ("lk", 128, 320), "alk", "hi")]))
        calls[q1].append((["lw"], [(o1, ("pk", 320, PK), ("lk", 320, PK), "ald", "hi")]))
        calls[o0].append((["lx"], [(q0, X, ("xr", 0, TK), "ax0", "h0"), (q1, X, ("xr", 0, TK), "ax0", "all")]))
        calls[o1].append((["lx"], [(q1, X, ("xr", TK, 2 * TK), "ax1", "h0"), (q0, X, ("xr", TK, 2 * TK), "ax1", "all")]))
        if root:
            calls[o0].append((["awr"], [(q1, U, U, "awu", "all")]))
            calls[o0].append(([], [(q1, V, V, "awv", "lo"), (o1, V, V, "awv", "up")]))
        else:
            calls[o0].append((["aw4"], [(q1, w, w, "aw4", "lo"), (o1, w, w, "aw4", "up")]))
        for q, o in ((q0, o0), (q1, o1)):
            t = reach(q)
            a, b, sem, wt = (("pp", 0, TK), ("pp", 0, TK), "app", "v5") if root else (("sb", 0, TK), ("b4", 0, TK), "ab4", "v2")
            calls[q].append(([wt], [(t[0], a, b, sem, "lo"), (t[1], a, b, sem, "up"), (o, a, b, sem, "hi")]))
    calls[relay].append((["awv"], [(far[1], V, V, "awv", "all"), (near_q, V, V, "awv", "hi")]))
    calls[relay].append(([], [(far[0], V, V, "awv", "all")]))
    return calls, far


def rank_program(g, core, T, topo):
    r = T.rank_of(core)
    if r is None:
        return
    cores = list(T.cores)
    S = T.sem
    calls, far = _plan(topo, cores)

    full = {s: 16 for s in LOADS}
    full.update({s: 1 for s in ONES})
    full.update({s: 0 for s in ARRIVALS})
    for src in calls:
        ln = _lanes(topo, cores, cores[src])
        for _, trs in calls[src]:
            for (dst, _, _, sem, lane) in trs:
                if dst == r:
                    full[sem] += len(ln[lane])

    queues = {"g": g, "t": g.tensor, "v": g.vector, "s": g.sync}
    seen = {}

    def need(q, sems):
        for s in sems:
            if (q, s) not in seen:
                seen[(q, s)] = True
                queues[q].wait_ge(S[s], full[s])

    def cols(name, c0, c1):
        return T[name][:, c0:c1]

    leader, q0, q1 = r % 2 == 0, r % 4 == 0, r % 4 == 2
    o1 = r % 4 == 3
    root_rack = topo.rack(topo.host(core)) == topo.rack(topo.host(cores[0]))
    d4 = far[0]
    X = T.xo[:]

    if q0:
        if r == 0:
            g.sync.dma_start(T.wr[:], T.wu[:, 512:768]).then_inc(S.lr, 16)
        else:
            g.sync.dma_start(T.w4[:], T.wd[:]).then_inc(S.lw, 16)
        g.scalar.dma_start(cols("pk", 320, PK), T.wu[:, 256:512]).then_inc(S.lv, 16)
        g.sync.dma_start(X, T.x[:]).then_inc(S.lx, 16)
        g.scalar.dma_start(cols("pk", 0, GC), T.wu[:, 0:256]).then_inc(S.lu, 16)
    elif q1:
        g.sync.dma_start(X, T.x[:]).then_inc(S.lx, 16)
        g.scalar.dma_start(cols("pk", 0, GC), T.wu[:, 0:256]).then_inc(S.lu, 16)
        g.sync.dma_start(cols("pk", 320, PK), T.wd[:]).then_inc(S.lw, 16)
    else:
        g.sync.dma_start(X, T.x[:]).then_inc(S.lx, 16)
        g.scalar.dma_start(cols("pk", 320, PK), T.wd[:]).then_inc(S.lw, 16)

    if leader:
        g.vector.memset(T.one[:], 1.0).then_inc(S.on1, 1)
        need("g", ["on1"])
        g.affine_select(T.idm[:], T.one[:], [[-1, 128]], AluOpType.is_equal, 0.0, 0, 1).then_inc(S.idn, 1)
    g.vector.memset(T.zz[:], 0.0).then_inc(S.zs, 1)
    seye = "idn" if leader else "aid"

    ln = _lanes(topo, cores, core)
    sent = 0
    for waits, trs in calls[r]:
        need("g", waits)
        lst = []
        for (dst, a, b, sem, lane) in trs:
            rid, pid = topo.addr(cores[dst], core)
            m = 0
            for e in ln[lane]:
                m |= 1 << e
            sent += len(ln[lane])
            lst.append(RemoteDMATransfer(dst_ids=[DstId(rid=rid, pnc=pid)], dma_engine_mask=m, remote_sem=S[sem],
                                         src=cols(*a), dst=cols(*b)))
        g.remote_dma_fused(lst, local_sem=S.sent)
    g.wait_ge(S.sent, sent)

    def mm(ps, lhsT, rhs, start, stop, waits, done=None):
        need("t", waits)
        i = g.tensor.matmul(T[ps][:, 0:TK], lhsT, rhs, start, stop)
        if done is not None:
            i.then_inc(S[done], 1)

    def relu(ps, out, msem, vsem):
        need("v", [msem, "zs"])
        g.vector.tensor_tensor(out, T[ps][:, 0:TK], T.zz[:], AluOpType.max).then_inc(S[vsem], 1)

    eye = T.idm[:]
    ownD, ownE = cols("pk", 320, 448), cols("pk", 448, PK)
    wrU, wrV = cols("wr", 0, 128), cols("wr", 128, 256)
    w4D, w4E = cols("w4", 0, 128), cols("w4", 128, 256)
    whole = "lr" if r == 0 else ("awr" if full["awr"] else None)
    swu, swv = whole or "awu", whole or "awv"
    sw4 = "lw" if r == d4 else "aw4"
    sb, pp, sc, d1, d2, yb = T.sb[:], T.pp[:], T.sc[:], T.d1[:], T.d2[:], T.yb[:]
    a_q1 = cols("sa", TK, 2 * TK)

    if leader:
        me, ot = (0, 1) if q0 else (1, 0)
        sa_me, sa_ot = cols("sa", me * TK, me * TK + TK), cols("sa", ot * TK, ot * TK + TK)
        l1, s1 = ("pk", "lv") if q0 else ("ol", "aob")
        U1, V1 = cols(l1, 320, 448), cols(l1, 448, PK)
        w_me, w_ot = (U1, V1) if q0 else (V1, U1)
        mm("p7", cols("pk", 0, 128), X, True, True, ["lx", "lu"], "mg")
        need("v", ["mg"])
        g.vector.tensor_copy(cols("pk", GC, GC + TK), T.p7[:, 0:TK]).then_inc(S.vg, 1)
        mm("p0", cols("pk", 0, 128), X, True, False, [])
        mm("p0", cols("pk", 128, 256), cols("xr", me * TK, me * TK + TK), False, True, ["ax%d" % me], "m0")
        relu("p0", sa_me, "m0", "v0")
        mm("p1", eye, cols("ol", GC, GC + TK), True, False, [seye, "aol"])
        mm("p1", cols("ol", 128, 256), cols("xr", ot * TK, ot * TK + TK), False, True, ["ax%d" % ot], "m1")
        relu("p1", sa_ot, "m1", "v1")
        mm("p2", w_me, sa_me, True, False, ["v0", s1])
        mm("p2", w_ot, sa_ot, False, True, ["v1"], "m2")
        relu("p2", sb, "m2", "v2")
        if root_rack:
            mm("p5", wrU, sb, True, True, ["v2", swu], "m5")
            need("v", ["m5"])
            g.vector.tensor_copy(pp, T.p5[:, 0:TK]).then_inc(S.v5, 1)
        if q1:
            mm("p6", ownD, a_q1, True, False, ["lw"])
    else:
        mm("p6", ownD, X, True, False, ["lx", "lw"])
    if o1:
        mm("p1", eye, cols("lk", GC, GC + TK), True, False, [seye, "alk"])
        mm("p1", cols("lk", 128, 256), X, False, True, [], "m1")
        relu("p1", a_q1, "m1", "v1")
        mm("p5", cols("lk", 320, 448), a_q1, True, False, ["v1", "ald"])

    own_b4 = leader and not root_rack
    b4, sb4 = (sb, "v2") if own_b4 else (T.b4[:], "ab4")
    if root_rack:
        if leader:
            mm("p3", wrU, sb, True, False, ["v2", swu])
        else:
            mm("p3", eye, pp, True, False, [seye, "app"])
        mm("p3", wrV, b4, False, True, [sb4, swv], "m3")
    else:
        mm("p3", wrV, b4, True, False, [sb4, swv])
        mm("p3", eye, pp, False, True, [seye, "app"], "m3")
    last = None
    if r == 0:
        relu("p3", yb, "m3", "vf")
    else:
        relu("p3", sc, "m3", "v3")
        last = (sc, "v3")
    if not root_rack:
        mm("p4", w4D, b4, True, False, [sw4])
        mm("p4", w4E, sc, False, True, ["v3"], "m4")
        if r == d4:
            relu("p4", yb, "m4", "vf")
            last = None
        else:
            relu("p4", d1, "m4", "v4")
            last = (d1, "v4")
    if o1:
        mm("p5", cols("lk", 448, PK), last[0], False, True, [last[1]], "m5")
        relu("p5", d2, "m5", "v5")
        last = (d2, "v5")
    if last is not None:
        mm("p6", ownE, last[0], False, True, [last[1]], "m6")
        relu("p6", yb, "m6", "vf")

    need("s", ["vf"])
    g.sync.dma_start(T.y[:], yb).then_inc(S.st, 16)
    g.sync.wait_ge(S.st, 16)
